import numpy as np
CORES = [13,21,141,149]
N = 4
T, CAPP = 1024, 512
def entries(a): return a.T.reshape(-1)
def pack(v, P): return np.ascontiguousarray(np.asarray(v, np.int32).reshape(-1, P).T)
def places(p):
    n = len(p); pl = [-1] * n; c = int(np.setdiff1d(np.arange(n), p[p != np.arange(n)])[:1].sum()); q = p.tolist()
    for k in range(n):
        if pl[c] >= 0: break
        pl[c] = k; c = q[c]
    return np.array(pl, np.int64)
def most(p):
    c = np.bincount(np.arange(N * T) // T * N + places(p) // T, minlength=N * N).reshape(N, N); return int((c - np.diag(np.diag(c))).max())
def deal(rng, m): return np.argsort(rng.random((N, m)), axis=1)
def lists(rng, how):
    n, i, G = N * T, np.arange(N), T // CAPP
    if how == "order": o = np.arange(n)
    elif how == "stride": o = np.lexsort((rng.random(n), np.arange(n) % 8))
    elif how == "mixed":
        a, t, m = rng.permutation(N), int(rng.integers(1, CAPP)), N - 1; z = a[m]; L = np.zeros((N, N), np.int64)
        for s in range(1, G + 1): L[a[:m], a[(i[:m] + s) % m]] = CAPP
        L[z, z], L[a[0], a[1]], L[a[0], z], L[z, a[1]] = T - t, CAPP - t, t, t
        lo, hi = np.zeros((N, N), np.int64), np.where(np.eye(N) > 0, T - CAPP, CAPP); lo[z, z], hi[z, z], lo[a[1], a[2]] = T - CAPP + 1, T - 1, CAPP
        for k in range(4 * N * N):
            r, u, d, v = np.append(rng.permutation(N)[:2], rng.permutation(N)[:2])
            t = int(rng.integers(0, 1 + min(hi[r, d] - L[r, d], hi[u, v] - L[u, v], L[r, v] - lo[r, v], L[u, d] - lo[u, d])))
            L[r, d] += t; L[u, v] += t; L[r, v] -= t; L[u, d] -= t
        o = np.lexsort((rng.random(n), np.concatenate([rng.permutation(np.repeat(i, l)) for l in L])))
    else:
        g, j = np.arange(G)[:, None], np.arange(CAPP)
        s = {"back": np.append(1 + np.arange(G - 1), N - 1), "full": 1 + np.arange(G), "hops": 1 + (G + np.arange(G)) % (N - 1)}[how]
        to = (i[:, None] + s) % N
        c, Q = deal(rng, T).reshape(N, G, CAPP), deal(rng, T).reshape(N, G, CAPP)
        if how == "hops": Q[:] = G * j + g
        if how == "back":
            c = np.sort(np.concatenate([np.full((N, 1), T - 1), 1 + deal(rng, T - 2), np.zeros((N, 1), np.int64)], axis=1).reshape(N, G, CAPP), axis=2); Q[:] = CAPP * g + j[::-1]
        o = np.empty(n, np.int64); o[T * to[:, :, None] + Q[to, g.T]] = T * i[:, None, None] + c
    p = np.empty(n, np.int64); p[o[:-1]] = o[1:]; p[o[-1]] = o[-1]
    return {"nx": np.stack([pack(v, 16) for v in p.reshape(N, T)])}
def setup_inputs(rng):
    return dict({"x": rng.standard_normal((N, 128, T), dtype=np.float32)}, **lists(rng, "mixed"))
def setup_inputs_back(rng):
    d = setup_inputs(rng); d.update(lists(rng, "back"))
    for k in ("x",): d[k] = (d[k].astype(np.float32) * 1048576.0).astype(d[k].dtype)
    return d
def setup_inputs_full(rng):
    d = setup_inputs(rng); d.update(lists(rng, "full"))
    for k in ("x",): d[k] = (d[k].astype(np.float32) * (1 / 1024.0)).astype(d[k].dtype)
    return d
def setup_inputs_hops(rng):
    d = setup_inputs(rng); d.update(lists(rng, "hops"))
    return d
def setup_inputs_order(rng):
    d = setup_inputs(rng); d.update(lists(rng, "order"))
    return d
def setup_inputs_stride(rng):
    d = setup_inputs(rng); d.update(lists(rng, "stride"))
    return d
def check_inputs(x):
    bad = []
    if x["nx"].min() < 0 or x["nx"].max() >= N * T: bad.append("nx out of range")
    if bad: return bad
    p = np.concatenate([entries(a) for a in x["nx"]])
    if (p == np.arange(N * T)).sum() != 1: bad.append("not exactly one column names itself")
    if not np.array_equal(np.sort(places(p)), np.arange(N * T)): bad.append("the line does not run through all columns, each once")
    elif most(p) > CAPP: bad.append("more than CAPP columns go from one rank's x to another rank's y")
    return bad
def reference(x, nx):
    X = np.concatenate(list(x), axis=1); p = np.concatenate([entries(a) for a in nx])
    pl = places(p); Y = np.zeros_like(X); Y[:, pl] = X
    return {"y": np.stack([Y[:, T * r:T * r + T] for r in range(N)])}

@@ -1,0 +1,386 @@
+from concourse.bass import DstId, RemoteDMATransfer
+from concourse.mybir import AluOpType as Op, AxisListType, ActivationFunctionType as Act
+
+W = 1024
+SCRATCH = {
+    "NXT": ("sbuf", [128, 128], "int32"),
+    "XALL": ("sbuf", [128, 4096], "float32"),
+    "YB": ("sbuf", [128, 1024], "float32"),
+    "IA": ("sbuf", [128, 512], "int32"),
+    "IQ": ("sbuf", [128, 512], "int32"),
+    "IP": ("sbuf", [128, 32], "int32"),
+    "MG": ("sbuf", [128, 128], "int32"),
+    "M8": ("sbuf", [128, 128], "int32"),
+    "MT": ("sbuf", [128, 128], "int32"),
+    "PF": ("sbuf", [128, 32], "float32"),
+    "EG": ("sbuf", [128, 8], "float32"),
+    "DM": ("sbuf", [128, 512], "float16"),
+    "BD": ("sbuf", [128, 128], "float16"),
+    "LG": ("sbuf", [128, 128], "float16"),
+    "BL": ("sbuf", [128, 128], "float16"),
+    "BW": ("sbuf", [128, 128], "float16"),
+    "T1": ("sbuf", [128, 128], "float16"),
+    "T2": ("sbuf", [128, 128], "float16"),
+    "T3": ("sbuf", [128, 128], "float16"),
+    "LW": ("sbuf", [128, 128], "float16"),
+    "LWL": ("sbuf", [128, 128], "float16"),
+    "LWH": ("sbuf", [128, 128], "float16"),
+    "SS": ("sbuf", [128, 128], "float16"),
+    "LQ": ("sbuf", [128, 2048], "float16"),
+    "LA": ("sbuf", [128, 2048], "float16"),
+    "SG": ("sbuf", [128, 1024], "float16"),
+    "ONE": ("sbuf", [128, 128], "float32"),
+    "EXP": ("sbuf", [128, 32], "uint16"),
+    "JI": ("sbuf", [128, 32], "float32"),
+    "P8X": ("sbuf", [128, 16], "float16"),
+    "WINA": ("sbuf", [128, 1024], "float32"),
+    "WINB": ("sbuf", [128, 1024], "float32"),
+    "VA": ("sbuf", [128, 32], "int32"),
+    "VB": ("sbuf", [128, 32], "int32"),
+    "VV": ("sbuf", [128, 32], "int32"),
+    "VH": ("sbuf", [128, 32], "int32"),
+    "VL": ("sbuf", [128, 32], "int32"),
+    "EQ": ("sbuf", [128, 32], "float32"),
+    "ET": ("sbuf", [128, 32], "float32"),
+    "ED": ("sbuf", [128, 32], "float32"),
+    "HS": ("sbuf", [128, 4], "float32"),
+    "HI": ("sbuf", [128, 4], "int32"),
+    "X": ("sbuf", [128, 640], "float16"),
+    "XE": ("sbuf", [128, 512], "float16"),
+    "M": ("sbuf", [128, 640], "float16"),
+    "OFF": ("sbuf", [128, 40], "uint16"),
+    "VF": ("sbuf", [128, 8], "float16"),
+    "OFY": ("sbuf", [128, 64], "uint16"),
+    "G0": ("psum", [128, 512], "float32"),
+    "G1": ("psum", [128, 512], "float32"),
+    "W0": ("psum", [128, 512], "float32"),
+    "W1": ("psum", [128, 512], "float32"),
+    "OF": ("psum", [128, 512], "float32"),
+    "GW": ("psum", [128, 512], "float32"),
+    "HD": ("psum", [128, 512], "float32"),
+}
+PSUM = [k for k in SCRATCH if SCRATCH[k][0] == "psum"]
+SEMAPHORES = ["cv", "cp", "ca", "cg", "nl", "x0", "x1", "x2", "x3", "nxp", "nxo", "hn", "hx", "xr", "ls", "ys"]
+NX_ENG = 4
+
+
+def engines(mask):
+    return [e for e in range(16) if mask >> e & 1]
+
+
+def bits(es):
+    return sum(1 << e for e in es)
+
+
+def helpers_of(rc, T, topo):
+    off = [o for o in T.cores if o != rc and not topo.may_write(rc, o)]
+    c0 = rc - rc % 8
+    cand = [c for c in range(c0, c0 + 8) if c != rc and topo.host(c) == topo.host(rc) and topo.chip(c) == topo.chip(rc)
+            and all(topo.may_write(c, o) for o in off)]
+    cand.sort(key=lambda c: (topo.die(c) != topo.die(rc), c))
+    direct = [o for o in T.cores if o != rc and topo.may_write(rc, o)]
+    return cand[:4], off, direct
+
+
+def dst_id(d, s, topo):
+    rid, pid = topo.addr(d, s)
+    return DstId(rid=rid, pnc=pid)
+
+
+def off_mask(core, dests, topo):
+    m = topo.mask(core, dests[0])
+    for d in dests:
+        m &= topo.mask(core, d)
+    return m
+
+
+def helper_program(g, core, T, topo, rc, k, off, direct):
+    r = T.rank_of(rc)
+    loc = 0
+    if k == 0:
+        g.wait_ge(T.sem["hn"], NX_ENG)
+        n = T.NXT[:, 32 * r:32 * r + 32]
+        g.remote_dma_fused([RemoteDMATransfer(dst_ids=[dst_id(o, core, topo) for o in off], dma_engine_mask=off_mask(core, off, topo),
+                                              remote_sem=T.sem["nxo"], srcs=[n], dsts=[n for o in off])], local_sem=T.sem["ls"])
+        loc += 8
+    dests = list(off)
+    if topo.die(core) != topo.die(rc):
+        dests += direct
+    q = T.XALL[:, 1024 * r + 256 * k:1024 * r + 256 * k + 256]
+    g.wait_ge(T.sem["hx"], 4)
+    g.remote_dma_fused([RemoteDMATransfer(dst_ids=[dst_id(o, core, topo) for o in dests], dma_engine_mask=off_mask(core, dests, topo),
+                                          remote_sem=T.sem["xr"], srcs=[q], dsts=[q for o in dests])], local_sem=T.sem["ls"])
+    loc += 8
+    g.wait_ge(T.sem["ls"], loc)
+
+
+def rank_program(g, core, T, topo):
+    rank = T.rank_of(core)
+    if rank is None:
+        for rc in T.cores:
+            hs, off, direct = helpers_of(rc, T, topo)
+            if core in hs:
+                helper_program(g, core, T, topo, rc, hs.index(core), off, direct)
+        return
+    r = rank
+    hs, off, direct = helpers_of(core, T, topo)
+    mate = direct[0]
+    rm = T.rank_of(mate)
+    ro = [T.rank_of(o) for o in off]
+    Q = {"v": g.vector, "p": g.tensor, "a": g.scalar, "g": g, "s": g.sync}
+    cnt = {"v": 0, "p": 0, "a": 0, "g": 0}
+    seen = {}
+    hist = {}
+
+    def need(q, sem, val):
+        if seen.get((q, sem), 0) < val:
+            Q[q].wait_ge(T.sem[sem], val)
+            seen[(q, sem)] = val
+
+    def op(q, call, rd, wr, ext=()):
+        nd = {}
+        for acc, iw in ((rd, False), (wr, True)):
+            for b, a0, a1 in acc:
+                for (c0, c1, w, e, n) in hist.get(b, ()):
+                    if b in PSUM:
+                        hit = e != q
+                    else:
+                        hit = c0 < a1 and a0 < c1 and ((w and not iw) or (iw and e != q))
+                    if hit and nd.get(e, 0) < n:
+                        nd[e] = n
+        for s, n in ext:
+            need(q, s, n)
+        for e in sorted(nd):
+            need(q, "c" + e, nd[e])
+        call().then_inc(T.sem["c" + q], 1)
+        cnt[q] += 1
+        for b, a0, a1 in wr:
+            if b in PSUM:
+                hist[b] = [h for h in hist.get(b, []) if h[3] != q] + [(a0, a1, True, q, cnt[q])]
+            else:
+                hist[b] = [h for h in hist.get(b, []) if not (a0 <= h[0] and h[1] <= a1)] + [(a0, a1, True, q, cnt[q])]
+        for b, a0, a1 in rd:
+            l = [h for h in hist.get(b, []) if not (h[2] is False and h[3] == q and a0 <= h[0] and h[1] <= a1)]
+            hist[b] = l + [(a0, a1, False, q, cnt[q])]
+
+    def at(b, a0, a1, step=1):
+        return T[b][:, a0:a1] if step == 1 else T[b][:, a0:a1:step]
+
+    def ts(out, i0, s1, s2, o0, o1=None, step=1, extra=()):
+        rd = [i0] + list(extra)
+        f = []
+        for s in (s1, s2):
+            if isinstance(s, tuple):
+                rd.append((s[0], s[1], s[1] + 1))
+                f.append(T[s[0]][:, s[1]:s[1] + 1])
+            else:
+                f.append(s)
+        if o1 is None:
+            op("v", lambda: g.vector.tensor_scalar(at(*out), at(*i0), f[0], f[1], o0), rd, [out])
+        else:
+            op("v", lambda: g.vector.tensor_scalar(at(*out), at(*i0), f[0], f[1], o0, o1), rd, [out])
+
+    def tt(out, i0, i1, o, ext=()):
+        op("v", lambda: g.vector.tensor_tensor(at(*out), at(*i0), at(*i1), o), [i0, i1], [out], ext)
+
+    def tc(out, i0):
+        op("v", lambda: g.vector.tensor_copy(at(*out), at(*i0)), [i0], [out])
+
+    def ms(out, c):
+        op("v", lambda: g.vector.memset(at(*out), c), [], [out])
+
+    def mm(out, lh, rh, st, sp, so=1, sr=1):
+        op("p", lambda: g.tensor.matmul(at(*out, so), at(*lh), at(*rh, sr), st, sp), [lh, rh], [out])
+
+    def ac(out, i0, scale=None, step=1):
+        if scale is None:
+            op("a", lambda: g.scalar.activation(at(*out, step), at(*i0, step), Act.Copy), [i0], [out])
+        else:
+            op("a", lambda: g.scalar.activation(at(*out, step), at(*i0, step), Act.Copy, scale=T[scale[0]][:, scale[1]:scale[1] + 1]),
+               [i0, (scale[0], scale[1], scale[1] + 1)], [out])
+
+    no = 32 * r
+    for e in range(2):
+        g.sync.dma_start(T.NXT[32 * r + 16 * e:32 * r + 16 * e + 16, no:no + 32], T.nx[:, 32 * e:32 * e + 32]).then_inc(T.sem["nl"], 16)
+    for k in range(4):
+        g.sync.dma_start(T.XALL[:, 1024 * r + 256 * k:1024 * r + 256 * k + 256], T.x[:, 256 * k:256 * k + 256]).then_inc(T.sem["x%d" % k], 16)
+    nz = 0
+    for p0, p1 in ((0, 64), (64, 128)):
+        if p0 <= 32 * r < p1:
+            o = 32 * r
+            p0, p1 = (o + 32, p1) if o == p0 else (p0, o)
+        g.vector.memset(T.NXT[p0:p1, no:no + 32], 0).then_inc(T.sem["cv"], 1)
+        cnt["v"] += 1
+        nz += 1
+    op("g", lambda: g.iota(at("IP", 0, 1), [[0, 1]], 0, 1), [], [("IP", 0, 1)])
+    op("g", lambda: g.iota(at("IA", 0, 512), [[1, 512]], 0, 0), [], [("IA", 0, 512)])
+    up = topo.mask(core, mate)
+    on = topo.mask(core, hs[0])
+    need("g", "nl", 32)
+    need("g", "cv", nz)
+    n = T.NXT[:, no:no + 32]
+    g.remote_dma_fused([
+        RemoteDMATransfer(dst_ids=[dst_id(hs[0], core, topo)], dma_engine_mask=bits(engines(on & ~up)[:NX_ENG]), remote_sem=T.sem["hn"], srcs=[n], dsts=[n]),
+        RemoteDMATransfer(dst_ids=[dst_id(mate, core, topo)], dma_engine_mask=bits(engines(up)[:NX_ENG]), remote_sem=T.sem["nxp"], srcs=[n], dsts=[n]),
+    ], local_sem=T.sem["ls"])
+    tr = []
+    for k in range(4):
+        need("g", "x%d" % k, 16)
+        q = T.XALL[:, 1024 * r + 256 * k:1024 * r + 256 * k + 256]
+        tr.append(RemoteDMATransfer(dst_ids=[dst_id(hs[k], core, topo)], dma_engine_mask=bits(engines(on)[4 * k:4 * k + 4]),
+                                    remote_sem=T.sem["hx"], srcs=[q], dsts=[q]))
+    g.remote_dma_fused(tr, local_sem=T.sem["ls"])
+    q = T.XALL[:, 1024 * r:1024 * r + 512]
+    g.remote_dma_fused([RemoteDMATransfer(dst_ids=[dst_id(mate, core, topo)], dma_engine_mask=up, remote_sem=T.sem["xr"], srcs=[q], dsts=[q])],
+                       local_sem=T.sem["ls"])
+    loc = 2 * NX_ENG + 16 + 8
+
+    ashr, band = Op.arith_shift_right, Op.bitwise_and
+    ts(("IP", 2, 3), ("IP", 0, 1), 4, None, ashr)
+    ts(("IP", 3, 4), ("IP", 0, 1), 15, None, band)
+    ts(("IP", 4, 5), ("IP", 0, 1), 7, None, band)
+    ts(("IP", 5, 6), ("IP", 0, 1), 3, 1, ashr, band)
+    for t in range(7):
+        ts(("IP", 8 + t, 9 + t), ("IP", 0, 1), t, 1, ashr, band)
+    tc(("PF", 0, 4), ("IP", 2, 6))
+    ts(("PF", 4, 5), ("PF", 3, 4), -1.0, 1.0, Op.mult, Op.add)
+    tt(("PF", 5, 6), ("PF", 3, 4), ("PF", 2, 3), Op.mult)
+    ts(("PF", 6, 7), ("PF", 3, 4), 511.0, 1.0, Op.mult, Op.add)
+    ts(("PF", 7, 8), ("PF", 0, 1), 512.0, ("PF", 1), Op.mult, Op.add)
+    ts(("PF", 8, 15), ("IP", 8, 15), -512.0, 512.0, Op.mult, Op.add)
+    ts(("IQ", 0, 512), ("IA", 0, 512), 15, None, band)
+    ts(("DM", 0, 512), ("IQ", 0, 512), ("PF", 1), None, Op.is_equal)
+    tc(("EXP", 0, 32), ("IA", 0, 32))
+    ts(("MG", 0, 128), ("IA", 0, 128), 4, None, ashr)
+    ts(("M8", 0, 128), ("IA", 0, 128), 7, None, band)
+    ts(("MT", 0, 128), ("IA", 0, 128), 3, 1, ashr, band)
+    ts(("BD", 0, 128), ("MG", 0, 128), ("PF", 0), None, Op.is_equal)
+    ts(("T1", 0, 128), ("M8", 0, 128), ("PF", 0), None, Op.is_equal)
+    ts(("T2", 0, 128), ("MT", 0, 128), ("PF", 3), None, Op.is_equal)
+    ts(("T3", 0, 128), ("MT", 0, 128), 0.0, None, Op.is_equal)
+    tt(("LWH", 0, 128), ("T1", 0, 128), ("MT", 0, 128), Op.mult)
+    tt(("LWL", 0, 128), ("T1", 0, 128), ("T3", 0, 128), Op.mult)
+    tt(("LW", 0, 128), ("T1", 0, 128), ("T2", 0, 128), Op.mult)
+    ts(("LG", 0, 128), ("MG", 0, 128), ("PF", 0), ("PF", 3), Op.is_equal, Op.mult)
+    ts(("BL", 0, 128), ("MG", 0, 128), ("PF", 0), ("PF", 4), Op.is_equal, Op.mult)
+    ms(("LQ", 0, 2048), 0.0)
+    ms(("LA", 0, 2048), 0.0)
+    ts(("BW", 0, 128), ("MG", 0, 128), ("PF", 0), ("PF", 6), Op.is_equal, Op.mult)
+    ts(("SS", 0, 128), ("IQ", 0, 128), ("PF", 1), None, Op.is_equal)
+    ts(("EG", 0, 8), ("IA", 0, 8), ("PF", 0), None, Op.is_equal)
+    ts(("JI", 0, 32), ("IA", 0, 32), 16.0, ("PF", 7), Op.mult, Op.add)
+    ts(("P8X", 0, 16), ("IA", 0, 16), 0.0, ("PF", 2), Op.mult, Op.add)
+    for w in ("WINA", "WINB"):
+        ts((w, 512, 1024), ("IA", 0, 512), ("PF", 4), ("PF", 5), Op.mult, Op.add)
+    ms(("ONE", 0, 128), 1.0)
+    for q in range(16):
+        op("a", lambda: g.scalar.activation(T.LQ[:, 128 * q + q:128 * q + 128:16], T.BL[:, q:128:16], Act.Copy),
+           [("BL", 0, 128)], [("LQ", 128 * q, 128 * q + 128)])
+    for q in range(16):
+        op("a", lambda: g.scalar.activation(T.LA[:, 128 * q + q:128 * q + 128:16], T.BW[:, q:128:16], Act.Copy),
+           [("BW", 0, 128)], [("LA", 128 * q, 128 * q + 128)])
+    for k in range(8):
+        ac(("SG", 128 * k, 128 * k + 128), ("SS", 0, 128), scale=("EG", k))
+
+    def blk(s):
+        return ("NXT", 32 * s, 32 * s + 32)
+    tt(("VA", 0, 32), blk(r), blk(rm), Op.add, ext=(("nl", 32), ("nxp", NX_ENG), ("cv", nz)))
+    tt(("VB", 0, 32), blk(ro[0]), blk(ro[1]), Op.add, ext=(("nxo", 16),))
+    tt(("VV", 0, 32), ("VA", 0, 32), ("VB", 0, 32), Op.add)
+    ts(("VH", 0, 32), ("VV", 0, 32), 9, None, ashr)
+    ts(("VL", 0, 32), ("VV", 0, 32), 511, None, band)
+
+    def gat(out, win, off, m):
+        op("v", lambda: g.vector.tensor_tensor(at(*out), T[win[0]][:, win[1]:win[2]].indirect(at(*off)), at(*m), Op.mult),
+           [win, off, m], [out])
+    gat(("X", 0, 512), ("VH", 0, 32), ("EXP", 0, 32), ("DM", 0, 512))
+    gat(("XE", 0, 512), ("VL", 0, 32), ("EXP", 0, 32), ("DM", 0, 512))
+    mm(("G0", 0, 512), ("BD", 0, 128), ("X", 0, 512), True, True)
+    mm(("W0", 0, 512), ("LWH", 0, 128), ("X", 0, 512), True, False)
+    mm(("W0", 0, 512), ("LWL", 0, 128), ("XE", 0, 512), False, True)
+    ac(("WINA", 0, 512), ("W0", 0, 512))
+    tt(("EQ", 0, 32), ("VV", 0, 32), ("JI", 0, 32), Op.is_equal)
+    tc(("OFF", 0, 32), ("VL", 0, 32))
+    tt(("ET", 0, 32), ("EQ", 0, 32), ("JI", 0, 32), Op.mult)
+    tt(("ED", 0, 32), ("VV", 0, 32), ("ET", 0, 32), Op.subtract)
+    op("v", lambda: g.vector.tensor_reduce(at("HS", 0, 1), at("ED", 0, 32), AxisListType.X, Op.add), [("ED", 0, 32)], [("HS", 0, 1)])
+    mm(("HD", 0, 1), ("ONE", 0, 128), ("HS", 0, 1), True, True)
+    ts(("M", 0, 512), ("G0", 0, 512), ("PF", 2), None, Op.is_equal)
+    ts(("HI", 0, 1), ("HD", 0, 1), -1.0, float(4096 * 4095 // 2), Op.mult, Op.add)
+    ts(("HI", 1, 2), ("HI", 0, 1), 9, None, ashr)
+    ts(("HI", 2, 3), ("HI", 0, 1), 511, None, band)
+    tc(("HS", 1, 2), ("HI", 1, 2))
+    ts(("OFF", 32, 33), ("HI", 2, 3), ("PF", 8), None, Op.add)
+    ts(("M", 512, 528), ("P8X", 0, 16), ("HS", 1), None, Op.is_equal)
+
+    cw = 1
+    for t in range(12):
+        win, nxt = (("WINA", "WINB") if t % 2 == 0 else ("WINB", "WINA"))
+        dbl, lst = t <= 10, t <= 9
+        wa, wb = 512, 512 + 16 * cw
+        if dbl:
+            gat(("X", 0, 256), (win, 0, 512), ("OFF", 0, 16), ("M", 0, 256))
+            gat(("X", 256, wb), (win, 0, 1024), ("OFF", 16, 32 + cw), ("M", 256, wb))
+        else:
+            gat(("X", wa, wb), (win, 0, 1024), ("OFF", 32, 32 + cw), ("M", wa, wb))
+        if lst:
+            mm(("G0", 0, 256), ("LG", 0, 128), ("X", 0, 256), True, True)
+        if dbl:
+            mm(("W0", 0, 256), ("LW", 0, 128), ("X", 0, 256), True, True)
+            ac((nxt, 0, 256), ("W0", 0, 256))
+        if lst:
+            mm(("G1", 0, 256), ("LG", 0, 128), ("X", 256, 512), True, True)
+            ts(("M", 0, 256), ("G0", 0, 256), ("PF", 2), None, Op.is_equal)
+        if dbl:
+            mm(("W1", 0, 256), ("LW", 0, 128), ("X", 256, 512), True, True)
+            ac((nxt, 256, 512), ("W1", 0, 256))
+        if lst:
+            ts(("M", 256, 512), ("G1", 0, 256), ("PF", 2), None, Op.is_equal)
+        if t == 11:
+            break
+        l0, n = (0, 32 + cw) if lst else (32, cw)
+        for q in range(16):
+            mm(("OF", l0, l0 + n), ("LQ", 128 * q, 128 * q + 128), ("X", 16 * l0 + q, wb), q == 0, q == 15, sr=16)
+        mm(("GW", 0, 16 * cw), ("LG", 0, 128), ("X", wa, wb), True, True)
+        if lst:
+            tc(("OFF", 0, 32), ("OF", 0, 32))
+        app = t in (7, 8, 9)
+        o = 32 + cw if app else 32
+        u = t + 1
+        hold = 512.0 if u >= 10 and not (r >> (u - 10) & 1) else 0.0
+        if u <= 6:
+            ts(("OFF", o, o + cw), ("OF", 32, 32 + cw), ("PF", 8 + u), None, Op.add)
+        else:
+            ts(("OFF", o, o + cw), ("OF", 32, 32 + cw), hold, None, Op.add)
+            if app and hold:
+                ts(("OFF", 32, 32 + cw), ("OFF", 32, 32 + cw), hold, None, Op.add)
+        mo = 512 + 16 * (o - 32)
+        ts(("M", mo, mo + 16 * cw), ("GW", 0, 16 * cw), ("PF", 2), None, Op.is_equal)
+        if app:
+            cw *= 2
+    for q in range(16):
+        mm(("OF", 0, 8), ("LA", 128 * q, 128 * q + 128), ("X", 512 + q, 640), q == 0, q == 15, sr=16)
+    ts(("VF", 0, 8), ("OF", 0, 8), -2048.0, None, Op.add)
+    for k in range(8):
+        mm(("HD", k, 64), ("SG", 128 * k, 128 * k + 128), ("VF", 0, 8), True, True, so=8)
+    ts(("OFY", 0, 64), ("HD", 0, 64), 2048.0, None, Op.add)
+    xs = (("x0", 16), ("x1", 16), ("x2", 16), ("x3", 16), ("xr", 8 * 3 + 8 * 4 * 2))
+    for c, q in ((0, "v"), (2, "a"), (1, "v"), (3, "a")):
+        a, b = 256 * c, 256 * c + 256
+        if q == "v":
+            op("v", lambda: g.vector.tensor_copy(T.YB[:, a:b], T.XALL[:, 0:4096].indirect(T.OFY[:, 16 * c:16 * c + 16])),
+               [("OFY", 0, 64)], [("YB", a, b)], xs)
+        else:
+            op("a", lambda: g.scalar.activation(T.YB[:, a:b], T.XALL[:, 0:4096].indirect(T.OFY[:, 16 * c:16 * c + 16]), Act.Copy),
+               [("OFY", 0, 64)], [("YB", a, b)], xs)
+        if c == 3:
+            need("a", "c" + q, cnt[q])
+            g.scalar.dma_start(T.y[:, a:b], T.YB[:, a:b]).then_inc(T.sem["ys"], 16)
+        else:
+            need("s", "c" + q, cnt[q])
+            g.sync.dma_start(T.y[:, a:b], T.YB[:, a:b]).then_inc(T.sem["ys"], 16)
+    g.wait_ge(T.sem["ls"], loc)
+    for e in "vpa":
+        need("g", "c" + e, cnt[e])
+    g.wait_ge(T.sem["cg"], cnt["g"])
+    g.wait_ge(T.sem["ys"], 64)

@@ -1,34 +1,42 @@
 from concourse.bass import DstId, RemoteDMATransfer
 from concourse.mybir import AluOpType as Op, AxisListType, ActivationFunctionType as Act
 
-W = 1024
 SCRATCH = {
     "NXT": ("sbuf", [128, 128], "int32"),
     "XALL": ("sbuf", [128, 4096], "float32"),
     "YB": ("sbuf", [128, 1024], "float32"),
-    "IA": ("sbuf", [128, 512], "int32"),
+    "IA": ("sbuf", [128, 128], "int32"),
+    "IL": ("sbuf", [128, 512], "int32"),
     "IQ": ("sbuf", [128, 512], "int32"),
     "IP": ("sbuf", [128, 32], "int32"),
     "MG": ("sbuf", [128, 128], "int32"),
     "M8": ("sbuf", [128, 128], "int32"),
     "MT": ("sbuf", [128, 128], "int32"),
+    "IM": ("sbuf", [128, 128], "int32"),
+    "K3": ("sbuf", [128, 128], "int32"),
     "PF": ("sbuf", [128, 32], "float32"),
     "EG": ("sbuf", [128, 8], "float32"),
+    "D0": ("sbuf", [128, 128], "float32"),
+    "S0": ("sbuf", [128, 64], "float32"),
+    "S1": ("sbuf", [128, 128], "float32"),
     "DM": ("sbuf", [128, 512], "float16"),
     "BD": ("sbuf", [128, 128], "float16"),
     "LG": ("sbuf", [128, 128], "float16"),
+    "LH": ("sbuf", [128, 128], "float16"),
     "BL": ("sbuf", [128, 128], "float16"),
-    "BW": ("sbuf", [128, 128], "float16"),
     "T1": ("sbuf", [128, 128], "float16"),
     "T2": ("sbuf", [128, 128], "float16"),
     "T3": ("sbuf", [128, 128], "float16"),
+    "SN": ("sbuf", [128, 128], "float16"),
     "LW": ("sbuf", [128, 128], "float16"),
+    "LV": ("sbuf", [128, 128], "float16"),
     "LWL": ("sbuf", [128, 128], "float16"),
     "LWH": ("sbuf", [128, 128], "float16"),
     "SS": ("sbuf", [128, 128], "float16"),
-    "LQ": ("sbuf", [128, 2048], "float16"),
-    "LA": ("sbuf", [128, 2048], "float16"),
+    "LQ": ("sbuf", [128, 512], "float16"),
+    "LP": ("sbuf", [128, 512], "float16"),
     "SG": ("sbuf", [128, 1024], "float16"),
+    "R8": ("sbuf", [128, 8], "float16"),
     "ONE": ("sbuf", [128, 128], "float32"),
     "EXP": ("sbuf", [128, 32], "uint16"),
     "JI": ("sbuf", [128, 32], "float32"),
@@ -55,8 +63,8 @@ SCRATCH = {
     "G1": ("psum", [128, 512], "float32"),
     "W0": ("psum", [128, 512], "float32"),
     "W1": ("psum", [128, 512], "float32"),
-    "OF": ("psum", [128, 512], "float32"),
-    "GW": ("psum", [128, 512], "float32"),
+    "OF0": ("psum", [128, 512], "float32"),
+    "OF1": ("psum", [128, 512], "float32"),
     "HD": ("psum", [128, 512], "float32"),
 }
 PSUM = [k for k in SCRATCH if SCRATCH[k][0] == "psum"]
@@ -166,8 +174,8 @@ def rank_program(g, core, T, topo):
     def at(b, a0, a1, step=1):
         return T[b][:, a0:a1] if step == 1 else T[b][:, a0:a1:step]
 
-    def ts(out, i0, s1, s2, o0, o1=None, step=1, extra=()):
-        rd = [i0] + list(extra)
+    def ts(out, i0, s1, s2, o0, o1=None, step=1):
+        rd = [i0]
         f = []
         for s in (s1, s2):
             if isinstance(s, tuple):
@@ -176,9 +184,9 @@ def rank_program(g, core, T, topo):
             else:
                 f.append(s)
         if o1 is None:
-            op("v", lambda: g.vector.tensor_scalar(at(*out), at(*i0), f[0], f[1], o0), rd, [out])
+            op("v", lambda: g.vector.tensor_scalar(at(*out), at(*i0, step), f[0], f[1], o0), rd, [out])
         else:
-            op("v", lambda: g.vector.tensor_scalar(at(*out), at(*i0), f[0], f[1], o0, o1), rd, [out])
+            op("v", lambda: g.vector.tensor_scalar(at(*out), at(*i0, step), f[0], f[1], o0, o1), rd, [out])
 
     def tt(out, i0, i1, o, ext=()):
         op("v", lambda: g.vector.tensor_tensor(at(*out), at(*i0), at(*i1), o), [i0, i1], [out], ext)
@@ -189,15 +197,15 @@ def rank_program(g, core, T, topo):
     def ms(out, c):
         op("v", lambda: g.vector.memset(at(*out), c), [], [out])
 
-    def mm(out, lh, rh, st, sp, so=1, sr=1):
-        op("p", lambda: g.tensor.matmul(at(*out, so), at(*lh), at(*rh, sr), st, sp), [lh, rh], [out])
+    def mm(out, lh, rh, st, sp, sr=1):
+        op("p", lambda: g.tensor.matmul(at(*out), at(*lh), at(*rh, sr), st, sp), [lh, rh], [out])
 
-    def ac(out, i0, scale=None, step=1):
-        if scale is None:
-            op("a", lambda: g.scalar.activation(at(*out, step), at(*i0, step), Act.Copy), [i0], [out])
-        else:
+    def ac(out, i0, scale=1.0, step=1):
+        if isinstance(scale, tuple):
             op("a", lambda: g.scalar.activation(at(*out, step), at(*i0, step), Act.Copy, scale=T[scale[0]][:, scale[1]:scale[1] + 1]),
                [i0, (scale[0], scale[1], scale[1] + 1)], [out])
+        else:
+            op("a", lambda: g.scalar.activation(at(*out, step), at(*i0, step), Act.Copy, scale=scale), [i0], [out])
 
     no = 32 * r
     for e in range(2):
@@ -213,7 +221,8 @@ def rank_program(g, core, T, topo):
         cnt["v"] += 1
         nz += 1
     op("g", lambda: g.iota(at("IP", 0, 1), [[0, 1]], 0, 1), [], [("IP", 0, 1)])
-    op("g", lambda: g.iota(at("IA", 0, 512), [[1, 512]], 0, 0), [], [("IA", 0, 512)])
+    op("g", lambda: g.iota(at("IA", 0, 128), [[1, 128]], 0, 0), [], [("IA", 0, 128)])
+    op("g", lambda: g.iota(at("IQ", 0, 512), [[0, 32], [1, 16]], 0, 0), [], [("IQ", 0, 512)])
     up = topo.mask(core, mate)
     on = topo.mask(core, hs[0])
     need("g", "nl", 32)
@@ -234,53 +243,79 @@ def rank_program(g, core, T, topo):
     g.remote_dma_fused([RemoteDMATransfer(dst_ids=[dst_id(mate, core, topo)], dma_engine_mask=up, remote_sem=T.sem["xr"], srcs=[q], dsts=[q])],
                        local_sem=T.sem["ls"])
     loc = 2 * NX_ENG + 16 + 8
+    op("g", lambda: g.iota(at("IL", 0, 512), [[1, 512]], 0, 0), [], [("IL", 0, 512)])
 
     ashr, band = Op.arith_shift_right, Op.bitwise_and
+    ms(("LQ", 0, 512), 0.0)
+    ms(("LP", 0, 512), 0.0)
+    ms(("ONE", 0, 128), 1.0)
     ts(("IP", 2, 3), ("IP", 0, 1), 4, None, ashr)
     ts(("IP", 3, 4), ("IP", 0, 1), 15, None, band)
     ts(("IP", 4, 5), ("IP", 0, 1), 7, None, band)
     ts(("IP", 5, 6), ("IP", 0, 1), 3, 1, ashr, band)
+    ts(("IP", 6, 7), ("IP", 0, 1), 2, 3, ashr, band)
     for t in range(7):
         ts(("IP", 8 + t, 9 + t), ("IP", 0, 1), t, 1, ashr, band)
-    tc(("PF", 0, 4), ("IP", 2, 6))
-    ts(("PF", 4, 5), ("PF", 3, 4), -1.0, 1.0, Op.mult, Op.add)
-    tt(("PF", 5, 6), ("PF", 3, 4), ("PF", 2, 3), Op.mult)
-    ts(("PF", 6, 7), ("PF", 3, 4), 511.0, 1.0, Op.mult, Op.add)
+    tc(("PF", 0, 5), ("IP", 2, 7))
+    tc(("EXP", 0, 32), ("IA", 0, 32))
+    ts(("PF", 5, 6), ("PF", 3, 4), -1.0, 1.0, Op.mult, Op.add)
+    ts(("PF", 17, 18), ("PF", 4, 5), -512.0, 1536.0, Op.mult, Op.add)
+    ts(("DM", 0, 512), ("IQ", 0, 512), ("PF", 1), None, Op.is_equal)
+    ts(("PF", 15, 16), ("PF", 2, 3), -1.0, 0.5, Op.mult, Op.add)
     ts(("PF", 7, 8), ("PF", 0, 1), 512.0, ("PF", 1), Op.mult, Op.add)
     ts(("PF", 8, 15), ("IP", 8, 15), -512.0, 512.0, Op.mult, Op.add)
-    ts(("IQ", 0, 512), ("IA", 0, 512), 15, None, band)
-    ts(("DM", 0, 512), ("IQ", 0, 512), ("PF", 1), None, Op.is_equal)
-    tc(("EXP", 0, 32), ("IA", 0, 32))
+    ts(("PF", 26, 27), ("PF", 2, 3), 0.0, 6.0, Op.is_equal, Op.mult)
+    ts(("PF", 25, 26), ("PF", 17, 18), 512.0, None, Op.add)
+    ts(("PF", 18, 25), ("PF", 8, 15), ("PF", 17), None, Op.add)
+    ts(("PF", 28, 29), ("PF", 26, 27), 1.0, ("PF", 3), Op.add, Op.mult)
+    ts(("PF", 27, 28), ("PF", 26, 27), 1.0 / 3.0, ("PF", 5), Op.mult, Op.mult)
+    ts(("PF", 29, 30), ("PF", 3, 4), 255.5, 0.5, Op.mult, Op.add)
     ts(("MG", 0, 128), ("IA", 0, 128), 4, None, ashr)
     ts(("M8", 0, 128), ("IA", 0, 128), 7, None, band)
+    ts(("IM", 0, 128), ("IA", 0, 128), 7.0, None, Op.add)
     ts(("MT", 0, 128), ("IA", 0, 128), 3, 1, ashr, band)
+    ts(("K3", 0, 128), ("IA", 0, 128), 3, None, band)
     ts(("BD", 0, 128), ("MG", 0, 128), ("PF", 0), None, Op.is_equal)
+    ts(("IM", 0, 128), ("IM", 0, 128), 7, None, band)
+    ts(("SN", 0, 128), ("M8", 0, 128), 0.0, 2.0, Op.is_equal, Op.mult)
+    ac(("BL", 0, 128), ("BD", 0, 128), scale=("PF", 5))
     ts(("T1", 0, 128), ("M8", 0, 128), ("PF", 0), None, Op.is_equal)
-    ts(("T2", 0, 128), ("MT", 0, 128), ("PF", 3), None, Op.is_equal)
-    ts(("T3", 0, 128), ("MT", 0, 128), 0.0, None, Op.is_equal)
+    ts(("SN", 0, 128), ("SN", 0, 128), -1.0, None, Op.add)
+    ts(("T2", 0, 128), ("IM", 0, 128), ("PF", 0), None, Op.is_equal)
+    ts(("T3", 0, 128), ("MT", 0, 128), ("PF", 3), None, Op.is_equal)
+    tt(("T2", 0, 128), ("T2", 0, 128), ("SN", 0, 128), Op.mult)
+    ac(("LG", 0, 128), ("BD", 0, 128), scale=("PF", 3))
+    tt(("T1", 0, 128), ("T1", 0, 128), ("T2", 0, 128), Op.add)
     tt(("LWH", 0, 128), ("T1", 0, 128), ("MT", 0, 128), Op.mult)
-    tt(("LWL", 0, 128), ("T1", 0, 128), ("T3", 0, 128), Op.mult)
-    tt(("LW", 0, 128), ("T1", 0, 128), ("T2", 0, 128), Op.mult)
-    ts(("LG", 0, 128), ("MG", 0, 128), ("PF", 0), ("PF", 3), Op.is_equal, Op.mult)
-    ts(("BL", 0, 128), ("MG", 0, 128), ("PF", 0), ("PF", 4), Op.is_equal, Op.mult)
-    ms(("LQ", 0, 2048), 0.0)
-    ms(("LA", 0, 2048), 0.0)
-    ts(("BW", 0, 128), ("MG", 0, 128), ("PF", 0), ("PF", 6), Op.is_equal, Op.mult)
-    ts(("SS", 0, 128), ("IQ", 0, 128), ("PF", 1), None, Op.is_equal)
-    ts(("EG", 0, 8), ("IA", 0, 8), ("PF", 0), None, Op.is_equal)
+    tt(("LW", 0, 128), ("T1", 0, 128), ("T3", 0, 128), Op.mult)
+    tt(("LWL", 0, 128), ("T1", 0, 128), ("LWH", 0, 128), Op.subtract)
+    ac(("LV", 0, 128), ("LW", 0, 128), scale=0.5)
+    ac(("LH", 0, 128), ("LG", 0, 128), scale=0.5)
+    ts(("D0", 0, 128), ("K3", 0, 128), ("PF", 4), 16896.0, Op.is_equal, Op.mult)
     ts(("JI", 0, 32), ("IA", 0, 32), 16.0, ("PF", 7), Op.mult, Op.add)
+    ts(("EG", 0, 8), ("IA", 0, 8), ("PF", 0), None, Op.is_equal)
+    ts(("D0", 0, 128), ("D0", 0, 128), -512.0, None, Op.add)
+    ts(("SS", 0, 128), ("IQ", 0, 128), ("PF", 1), None, Op.is_equal)
     ts(("P8X", 0, 16), ("IA", 0, 16), 0.0, ("PF", 2), Op.mult, Op.add)
-    for w in ("WINA", "WINB"):
-        ts((w, 512, 1024), ("IA", 0, 512), ("PF", 4), ("PF", 5), Op.mult, Op.add)
-    ms(("ONE", 0, 128), 1.0)
-    for q in range(16):
-        op("a", lambda: g.scalar.activation(T.LQ[:, 128 * q + q:128 * q + 128:16], T.BL[:, q:128:16], Act.Copy),
-           [("BL", 0, 128)], [("LQ", 128 * q, 128 * q + 128)])
-    for q in range(16):
-        op("a", lambda: g.scalar.activation(T.LA[:, 128 * q + q:128 * q + 128:16], T.BW[:, q:128:16], Act.Copy),
-           [("BW", 0, 128)], [("LA", 128 * q, 128 * q + 128)])
+    ts(("R8", 0, 8), ("EG", 0, 8), ("PF", 29), None, Op.mult)
+    ts(("WINA", 512, 1024), ("IL", 0, 512), ("PF", 27), ("PF", 28), Op.mult, Op.add)
+    for b, f in (("LQ", 1.0), ("LP", 0.5)):
+        for k in range(4):
+            op("a", lambda: g.scalar.activation(T[b][:, 128 * k + k:128 * k + 128:4], T.BL[:, k:128:4], Act.Copy, scale=f),
+               [("BL", 0, 128)], [(b, 128 * k, 128 * k + 128)])
     for k in range(8):
         ac(("SG", 128 * k, 128 * k + 128), ("SS", 0, 128), scale=("EG", k))
+    ac(("WINB", 512, 1024), ("WINA", 512, 1024))
+
+    def gat(out, win, off, m):
+        op("v", lambda: g.vector.tensor_tensor(at(*out), T[win[0]][:, win[1]:win[2]].indirect(at(*off)), at(*m), Op.mult),
+           [win, off, m], [out])
+
+    def mask0(out, i0):
+        ts(out, i0, ("PF", 2), 0.5, Op.is_ge, Op.subtract)
+
+    def mask1(out, i0):
+        op("a", lambda: g.scalar.activation(at(*out), at(*i0), Act.Sign, bias=T.PF[:, 15:16]), [i0, ("PF", 15, 16)], [out])
 
     def blk(s):
         return ("NXT", 32 * s, 32 * s + 32)
@@ -289,81 +324,103 @@ def rank_program(g, core, T, topo):
     tt(("VV", 0, 32), ("VA", 0, 32), ("VB", 0, 32), Op.add)
     ts(("VH", 0, 32), ("VV", 0, 32), 9, None, ashr)
     ts(("VL", 0, 32), ("VV", 0, 32), 511, None, band)
-
-    def gat(out, win, off, m):
-        op("v", lambda: g.vector.tensor_tensor(at(*out), T[win[0]][:, win[1]:win[2]].indirect(at(*off)), at(*m), Op.mult),
-           [win, off, m], [out])
-    gat(("X", 0, 512), ("VH", 0, 32), ("EXP", 0, 32), ("DM", 0, 512))
-    gat(("XE", 0, 512), ("VL", 0, 32), ("EXP", 0, 32), ("DM", 0, 512))
-    mm(("G0", 0, 512), ("BD", 0, 128), ("X", 0, 512), True, True)
-    mm(("W0", 0, 512), ("LWH", 0, 128), ("X", 0, 512), True, False)
-    mm(("W0", 0, 512), ("LWL", 0, 128), ("XE", 0, 512), False, True)
-    ac(("WINA", 0, 512), ("W0", 0, 512))
     tt(("EQ", 0, 32), ("VV", 0, 32), ("JI", 0, 32), Op.is_equal)
-    tc(("OFF", 0, 32), ("VL", 0, 32))
+    gat(("X", 0, 512), ("VH", 0, 32), ("EXP", 0, 32), ("DM", 0, 512))
     tt(("ET", 0, 32), ("EQ", 0, 32), ("JI", 0, 32), Op.mult)
+    tc(("OFF", 0, 32), ("VL", 0, 32))
+    gat(("XE", 0, 256), ("VL", 0, 32), ("EXP", 0, 16), ("DM", 0, 256))
     tt(("ED", 0, 32), ("VV", 0, 32), ("ET", 0, 32), Op.subtract)
+    gat(("XE", 256, 512), ("VL", 0, 32), ("EXP", 16, 32), ("DM", 256, 512))
     op("v", lambda: g.vector.tensor_reduce(at("HS", 0, 1), at("ED", 0, 32), AxisListType.X, Op.add), [("ED", 0, 32)], [("HS", 0, 1)])
+    for c in (1, 0):
+        mm(("G%d" % c, 0, 256), ("BD", 0, 128), ("X", 256 * c, 256 * c + 256), True, True)
+    for c in range(2):
+        mm(("W%d" % c, 0, 256), ("LWH", 0, 128), ("X", 256 * c, 256 * c + 256), True, False)
+    for c in range(2):
+        mm(("W%d" % c, 0, 256), ("LWL", 0, 128), ("XE", 256 * c, 256 * c + 256), False, True)
     mm(("HD", 0, 1), ("ONE", 0, 128), ("HS", 0, 1), True, True)
-    ts(("M", 0, 512), ("G0", 0, 512), ("PF", 2), None, Op.is_equal)
+    mask1(("M", 256, 512), ("G1", 0, 256))
+    for c in range(2):
+        ac(("WINA", 256 * c, 256 * c + 256), ("W%d" % c, 0, 256))
+    mask0(("M", 0, 256), ("G0", 0, 256))
     ts(("HI", 0, 1), ("HD", 0, 1), -1.0, float(4096 * 4095 // 2), Op.mult, Op.add)
     ts(("HI", 1, 2), ("HI", 0, 1), 9, None, ashr)
     ts(("HI", 2, 3), ("HI", 0, 1), 511, None, band)
-    tc(("HS", 1, 2), ("HI", 1, 2))
+    ts(("HS", 1, 2), ("HI", 1, 2), 0.5, None, Op.add)
     ts(("OFF", 32, 33), ("HI", 2, 3), ("PF", 8), None, Op.add)
-    ts(("M", 512, 528), ("P8X", 0, 16), ("HS", 1), None, Op.is_equal)
+    op("a", lambda: g.scalar.activation(T.M[:, 512:528], T.P8X[:, 0:16], Act.Sign, bias=T.HS[:, 1:2], scale=-1.0),
+       [("P8X", 0, 16), ("HS", 1, 2)], [("M", 512, 528)])
+
+    def sums(i, a, b, lq):
+        for k in range(4):
+            mm(("OF%d" % i, 0, (b - a) // 4), (lq, 128 * k, 128 * k + 128), ("X", a + k, b), k == 0, k == 3, sr=4)
+
+    def scan(i, n):
+        op("v", lambda: g.vector.tensor_tensor_scan(at("S%d" % i, 0, n), at("D0", 0, n), at("OF%d" % i, 0, n), 0.0, Op.add, Op.min),
+           [("D0", 0, n), ("OF%d" % i, 0, n)], [("S%d" % i, 0, n)])
+
+    def pick(i, c0, c1, o0, col):
+        op("v", lambda: g.vector.tensor_scalar(at("OFF", o0, o0 + c1 - c0), at("S%d" % i, 4 * c0 + 3, 4 * c1, 4), at("PF", col, col + 1), None, Op.add),
+           [("S%d" % i, 4 * c0, 4 * c1), ("PF", col, col + 1)], [("OFF", o0, o0 + c1 - c0)])
 
     cw = 1
     for t in range(12):
         win, nxt = (("WINA", "WINB") if t % 2 == 0 else ("WINB", "WINA"))
-        dbl, lst = t <= 10, t <= 9
-        wa, wb = 512, 512 + 16 * cw
-        if dbl:
-            gat(("X", 0, 256), (win, 0, 512), ("OFF", 0, 16), ("M", 0, 256))
-            gat(("X", 256, wb), (win, 0, 1024), ("OFF", 16, 32 + cw), ("M", 256, wb))
-        else:
-            gat(("X", wa, wb), (win, 0, 1024), ("OFF", 32, 32 + cw), ("M", wa, wb))
-        if lst:
-            mm(("G0", 0, 256), ("LG", 0, 128), ("X", 0, 256), True, True)
-        if dbl:
-            mm(("W0", 0, 256), ("LW", 0, 128), ("X", 0, 256), True, True)
-            ac((nxt, 0, 256), ("W0", 0, 256))
-        if lst:
-            mm(("G1", 0, 256), ("LG", 0, 128), ("X", 256, 512), True, True)
-            ts(("M", 0, 256), ("G0", 0, 256), ("PF", 2), None, Op.is_equal)
-        if dbl:
-            mm(("W1", 0, 256), ("LW", 0, 128), ("X", 256, 512), True, True)
-            ac((nxt, 256, 512), ("W1", 0, 256))
-        if lst:
-            ts(("M", 256, 512), ("G1", 0, 256), ("PF", 2), None, Op.is_equal)
-        if t == 11:
-            break
-        l0, n = (0, 32 + cw) if lst else (32, cw)
-        for q in range(16):
-            mm(("OF", l0, l0 + n), ("LQ", 128 * q, 128 * q + 128), ("X", 16 * l0 + q, wb), q == 0, q == 15, sr=16)
-        mm(("GW", 0, 16 * cw), ("LG", 0, 128), ("X", wa, wb), True, True)
-        if lst:
-            tc(("OFF", 0, 32), ("OF", 0, 32))
+        wb = 512 + 16 * cw
         app = t in (7, 8, 9)
         o = 32 + cw if app else 32
-        u = t + 1
-        hold = 512.0 if u >= 10 and not (r >> (u - 10) & 1) else 0.0
-        if u <= 6:
-            ts(("OFF", o, o + cw), ("OF", 32, 32 + cw), ("PF", 8 + u), None, Op.add)
-        else:
-            ts(("OFF", o, o + cw), ("OF", 32, 32 + cw), hold, None, Op.add)
-            if app and hold:
-                ts(("OFF", 32, 32 + cw), ("OFF", 32, 32 + cw), hold, None, Op.add)
         mo = 512 + 16 * (o - 32)
-        ts(("M", mo, mo + 16 * cw), ("GW", 0, 16 * cw), ("PF", 2), None, Op.is_equal)
+        u = t + 1
+        hold = u >= 10 and not (r >> (u - 10) & 1)
+        wcol = 18 + u if u <= 6 else 25 if hold else 17
+        if t == 11:
+            gat(("X", 512, wb), (win, 0, 1024), ("OFF", 32, 32 + cw), ("M", 512, wb))
+            break
+        gat(("X", 0, 256), (win, 0, 512), ("OFF", 0, 16), ("M", 0, 256))
+        if t == 10:
+            gat(("X", 256, 512), (win, 0, 512), ("OFF", 16, 32), ("M", 256, 512))
+            gat(("X", 512, wb), (win, 0, 1024), ("OFF", 32, 32 + cw), ("M", 512, wb))
+            mm(("W0", 0, 256), ("LW", 0, 128), ("X", 0, 256), True, True)
+            ac((nxt, 0, 256), ("W0", 0, 256))
+            mm(("W1", 0, 256), ("LV", 0, 128), ("X", 256, 512), True, True)
+            ac((nxt, 256, 512), ("W1", 0, 256))
+            sums(1, 512, wb, "LP")
+            mm(("G1", 0, wb - 512), ("LH", 0, 128), ("X", 512, wb), True, True)
+            scan(1, 4 * cw)
+            mask1(("M", 512, wb), ("G1", 0, wb - 512))
+            pick(1, 0, cw, 32, wcol)
+            continue
+        gat(("X", 256, wb), (win, 0, 1024), ("OFF", 16, 32 + cw), ("M", 256, wb))
+        mm(("W0", 0, 256), ("LW", 0, 128), ("X", 0, 256), True, True)
+        sums(0, 0, 256, "LQ")
+        mm(("G0", 0, 256), ("LG", 0, 128), ("X", 0, 256), True, True)
+        mm(("W1", 0, 256), ("LV", 0, 128), ("X", 256, 512), True, True)
+        sums(1, 256, wb, "LP")
+        mm(("G1", 0, wb - 256), ("LH", 0, 128), ("X", 256, wb), True, True)
+        ac((nxt, 0, 256), ("W0", 0, 256))
+        ac((nxt, 256, 512), ("W1", 0, 256))
+        scan(0, 64)
+        mask0(("M", 0, 256), ("G0", 0, 256))
+        scan(1, (wb - 256) // 4)
+        pick(0, 0, 16, 0, 17)
+        if wcol == 17 and o == 32:
+            pick(1, 0, 16 + cw, 16, 17)
+        else:
+            pick(1, 0, 16, 16, 17)
+            pick(1, 16, 16 + cw, o, wcol)
+        if app and hold:
+            ts(("OFF", 32, 32 + cw), ("OFF", 32, 32 + cw), 512.0, None, Op.add)
         if app:
+            mask1(("M", 256, 512), ("G1", 0, 256))
+            mask1(("M", mo, mo + 16 * cw), ("G1", 256, 256 + 16 * cw))
             cw *= 2
-    for q in range(16):
-        mm(("OF", 0, 8), ("LA", 128 * q, 128 * q + 128), ("X", 512 + q, 640), q == 0, q == 15, sr=16)
-    ts(("VF", 0, 8), ("OF", 0, 8), -2048.0, None, Op.add)
+        else:
+            mask1(("M", 256, wb), ("G1", 0, wb - 256))
+    mm(("HD", 0, 8), ("X", 512, 640), ("R8", 0, 8), True, True)
+    ts(("VF", 0, 8), ("HD", 0, 8), -2048.0, None, Op.add)
     for k in range(8):
-        mm(("HD", k, 64), ("SG", 128 * k, 128 * k + 128), ("VF", 0, 8), True, True, so=8)
-    ts(("OFY", 0, 64), ("HD", 0, 64), 2048.0, None, Op.add)
+        mm(("G0", 8 * k, 8 * k + 8), ("SG", 128 * k, 128 * k + 128), ("VF", 0, 8), True, True)
+    ts(("OFY", 0, 64), ("G0", 0, 64), 2048.0, None, Op.add)
     xs = (("x0", 16), ("x1", 16), ("x2", 16), ("x3", 16), ("xr", 8 * 3 + 8 * 4 * 2))
     for c, q in ((0, "v"), (2, "a"), (1, "v"), (3, "a")):
         a, b = 256 * c, 256 * c + 256

from concourse.bass import DstId, RemoteDMATransfer
from concourse.mybir import AluOpType as Op, AxisListType, ActivationFunctionType as Act

SCRATCH = {
    "NXT": ("sbuf", [128, 128], "int32"),
    "XALL": ("sbuf", [128, 4096], "float32"),
    "YB": ("sbuf", [128, 1024], "float32"),
    "IA": ("sbuf", [128, 128], "int32"),
    "IL": ("sbuf", [128, 512], "int32"),
    "IQ": ("sbuf", [128, 512], "int32"),
    "IP": ("sbuf", [128, 32], "int32"),
    "MG": ("sbuf", [128, 128], "int32"),
    "M8": ("sbuf", [128, 128], "int32"),
    "MT": ("sbuf", [128, 128], "int32"),
    "IM": ("sbuf", [128, 128], "int32"),
    "K3": ("sbuf", [128, 128], "int32"),
    "PF": ("sbuf", [128, 32], "float32"),
    "EG": ("sbuf", [128, 8], "float32"),
    "D0": ("sbuf", [128, 128], "float32"),
    "S0": ("sbuf", [128, 64], "float32"),
    "S1": ("sbuf", [128, 128], "float32"),
    "DM": ("sbuf", [128, 512], "float16"),
    "BD": ("sbuf", [128, 128], "float16"),
    "LG": ("sbuf", [128, 128], "float16"),
    "LH": ("sbuf", [128, 128], "float16"),
    "BL": ("sbuf", [128, 128], "float16"),
    "T1": ("sbuf", [128, 128], "float16"),
    "T2": ("sbuf", [128, 128], "float16"),
    "T3": ("sbuf", [128, 128], "float16"),
    "SN": ("sbuf", [128, 128], "float16"),
    "LW": ("sbuf", [128, 128], "float16"),
    "LV": ("sbuf", [128, 128], "float16"),
    "LWL": ("sbuf", [128, 128], "float16"),
    "LWH": ("sbuf", [128, 128], "float16"),
    "SS": ("sbuf", [128, 128], "float16"),
    "LQ": ("sbuf", [128, 512], "float16"),
    "LP": ("sbuf", [128, 512], "float16"),
    "SG": ("sbuf", [128, 1024], "float16"),
    "R8": ("sbuf", [128, 8], "float16"),
    "ONE": ("sbuf", [128, 128], "float32"),
    "EXP": ("sbuf", [128, 32], "uint16"),
    "JI": ("sbuf", [128, 32], "float32"),
    "P8X": ("sbuf", [128, 16], "float16"),
    "WINA": ("sbuf", [128, 1024], "float32"),
    "WINB": ("sbuf", [128, 1024], "float32"),
    "VA": ("sbuf", [128, 32], "int32"),
    "VB": ("sbuf", [128, 32], "int32"),
    "VV": ("sbuf", [128, 32], "int32"),
    "VH": ("sbuf", [128, 32], "int32"),
    "VL": ("sbuf", [128, 32], "int32"),
    "EQ": ("sbuf", [128, 32], "float32"),
    "ET": ("sbuf", [128, 32], "float32"),
    "ED": ("sbuf", [128, 32], "float32"),
    "HS": ("sbuf", [128, 4], "float32"),
    "HI": ("sbuf", [128, 4], "int32"),
    "X": ("sbuf", [128, 640], "float16"),
    "XE": ("sbuf", [128, 512], "float16"),
    "M": ("sbuf", [128, 640], "float16"),
    "OFF": ("sbuf", [128, 40], "uint16"),
    "VF": ("sbuf", [128, 8], "float16"),
    "OFY": ("sbuf", [128, 64], "uint16"),
    "G0": ("psum", [128, 512], "float32"),
    "G1": ("psum", [128, 512], "float32"),
    "W0": ("psum", [128, 512], "float32"),
    "W1": ("psum", [128, 512], "float32"),
    "OF0": ("psum", [128, 512], "float32"),
    "OF1": ("psum", [128, 512], "float32"),
    "HD": ("psum", [128, 512], "float32"),
}
PSUM = [k for k in SCRATCH if SCRATCH[k][0] == "psum"]
SEMAPHORES = ["cv", "cp", "ca", "cg", "nl", "x0", "x1", "x2", "x3", "nxp", "nxo", "hn", "hx", "xr", "ls", "ys"]
NX_ENG = 4


def engines(mask):
    return [e for e in range(16) if mask >> e & 1]


def bits(es):
    return sum(1 << e for e in es)


def helpers_of(rc, T, topo):
    off = [o for o in T.cores if o != rc and not topo.may_write(rc, o)]
    c0 = rc - rc % 8
    cand = [c for c in range(c0, c0 + 8) if c != rc and topo.host(c) == topo.host(rc) and topo.chip(c) == topo.chip(rc)
            and all(topo.may_write(c, o) for o in off)]
    cand.sort(key=lambda c: (topo.die(c) != topo.die(rc), c))
    direct = [o for o in T.cores if o != rc and topo.may_write(rc, o)]
    return cand[:4], off, direct


def dst_id(d, s, topo):
    rid, pid = topo.addr(d, s)
    return DstId(rid=rid, pnc=pid)


def off_mask(core, dests, topo):
    m = topo.mask(core, dests[0])
    for d in dests:
        m &= topo.mask(core, d)
    return m


def helper_program(g, core, T, topo, rc, k, off, direct):
    r = T.rank_of(rc)
    loc = 0
    if k == 0:
        g.wait_ge(T.sem["hn"], NX_ENG)
        n = T.NXT[:, 32 * r:32 * r + 32]
        g.remote_dma_fused([RemoteDMATransfer(dst_ids=[dst_id(o, core, topo) for o in off], dma_engine_mask=off_mask(core, off, topo),
                                              remote_sem=T.sem["nxo"], srcs=[n], dsts=[n for o in off])], local_sem=T.sem["ls"])
        loc += 8
    dests = list(off)
    if topo.die(core) != topo.die(rc):
        dests += direct
    q = T.XALL[:, 1024 * r + 256 * k:1024 * r + 256 * k + 256]
    g.wait_ge(T.sem["hx"], 4)
    g.remote_dma_fused([RemoteDMATransfer(dst_ids=[dst_id(o, core, topo) for o in dests], dma_engine_mask=off_mask(core, dests, topo),
                                          remote_sem=T.sem["xr"], srcs=[q], dsts=[q for o in dests])], local_sem=T.sem["ls"])
    loc += 8
    g.wait_ge(T.sem["ls"], loc)


def rank_program(g, core, T, topo):
    rank = T.rank_of(core)
    if rank is None:
        for rc in T.cores:
            hs, off, direct = helpers_of(rc, T, topo)
            if core in hs:
                helper_program(g, core, T, topo, rc, hs.index(core), off, direct)
        return
    r = rank
    hs, off, direct = helpers_of(core, T, topo)
    mate = direct[0]
    rm = T.rank_of(mate)
    ro = [T.rank_of(o) for o in off]
    Q = {"v": g.vector, "p": g.tensor, "a": g.scalar, "g": g, "s": g.sync}
    cnt = {"v": 0, "p": 0, "a": 0, "g": 0}
    seen = {}
    hist = {}

    def need(q, sem, val):
        if seen.get((q, sem), 0) < val:
            Q[q].wait_ge(T.sem[sem], val)
            seen[(q, sem)] = val

    def op(q, call, rd, wr, ext=()):
        nd = {}
        for acc, iw in ((rd, False), (wr, True)):
            for b, a0, a1 in acc:
                for (c0, c1, w, e, n) in hist.get(b, ()):
                    if b in PSUM:
                        hit = e != q
                    else:
                        hit = c0 < a1 and a0 < c1 and ((w and not iw) or (iw and e != q))
                    if hit and nd.get(e, 0) < n:
                        nd[e] = n
        for s, n in ext:
            need(q, s, n)
        for e in sorted(nd):
            need(q, "c" + e, nd[e])
        call().then_inc(T.sem["c" + q], 1)
        cnt[q] += 1
        for b, a0, a1 in wr:
            if b in PSUM:
                hist[b] = [h for h in hist.get(b, []) if h[3] != q] + [(a0, a1, True, q, cnt[q])]
            else:
                hist[b] = [h for h in hist.get(b, []) if not (a0 <= h[0] and h[1] <= a1)] + [(a0, a1, True, q, cnt[q])]
        for b, a0, a1 in rd:
            l = [h for h in hist.get(b, []) if not (h[2] is False and h[3] == q and a0 <= h[0] and h[1] <= a1)]
            hist[b] = l + [(a0, a1, False, q, cnt[q])]

    def at(b, a0, a1, step=1):
        return T[b][:, a0:a1] if step == 1 else T[b][:, a0:a1:step]

    def ts(out, i0, s1, s2, o0, o1=None, step=1):
        rd = [i0]
        f = []
        for s in (s1, s2):
            if isinstance(s, tuple):
                rd.append((s[0], s[1], s[1] + 1))
                f.append(T[s[0]][:, s[1]:s[1] + 1])
            else:
                f.append(s)
        if o1 is None:
            op("v", lambda: g.vector.tensor_scalar(at(*out), at(*i0, step), f[0], f[1], o0), rd, [out])
        else:
            op("v", lambda: g.vector.tensor_scalar(at(*out), at(*i0, step), f[0], f[1], o0, o1), rd, [out])

    def tt(out, i0, i1, o, ext=()):
        op("v", lambda: g.vector.tensor_tensor(at(*out), at(*i0), at(*i1), o), [i0, i1], [out], ext)

    def tc(out, i0):
        op("v", lambda: g.vector.tensor_copy(at(*out), at(*i0)), [i0], [out])

    def ms(out, c):
        op("v", lambda: g.vector.memset(at(*out), c), [], [out])

    def mm(out, lh, rh, st, sp, sr=1):
        op("p", lambda: g.tensor.matmul(at(*out), at(*lh), at(*rh, sr), st, sp), [lh, rh], [out])

    def ac(out, i0, scale=1.0, step=1):
        if isinstance(scale, tuple):
            op("a", lambda: g.scalar.activation(at(*out, step), at(*i0, step), Act.Copy, scale=T[scale[0]][:, scale[1]:scale[1] + 1]),
               [i0, (scale[0], scale[1], scale[1] + 1)], [out])
        else:
            op("a", lambda: g.scalar.activation(at(*out, step), at(*i0, step), Act.Copy, scale=scale), [i0], [out])

    no = 32 * r
    for e in range(2):
        g.sync.dma_start(T.NXT[32 * r + 16 * e:32 * r + 16 * e + 16, no:no + 32], T.nx[:, 32 * e:32 * e + 32]).then_inc(T.sem["nl"], 16)
    for k in range(4):
        g.sync.dma_start(T.XALL[:, 1024 * r + 256 * k:1024 * r + 256 * k + 256], T.x[:, 256 * k:256 * k + 256]).then_inc(T.sem["x%d" % k], 16)
    nz = 0
    for p0, p1 in ((0, 64), (64, 128)):
        if p0 <= 32 * r < p1:
            o = 32 * r
            p0, p1 = (o + 32, p1) if o == p0 else (p0, o)
        g.vector.memset(T.NXT[p0:p1, no:no + 32], 0).then_inc(T.sem["cv"], 1)
        cnt["v"] += 1
        nz += 1
    op("g", lambda: g.iota(at("IP", 0, 1), [[0, 1]], 0, 1), [], [("IP", 0, 1)])
    op("g", lambda: g.iota(at("IA", 0, 128), [[1, 128]], 0, 0), [], [("IA", 0, 128)])
    op("g", lambda: g.iota(at("IQ", 0, 512), [[0, 32], [1, 16]], 0, 0), [], [("IQ", 0, 512)])
    up = topo.mask(core, mate)
    on = topo.mask(core, hs[0])
    need("g", "nl", 32)
    need("g", "cv", nz)
    n = T.NXT[:, no:no + 32]
    g.remote_dma_fused([
        RemoteDMATransfer(dst_ids=[dst_id(hs[0], core, topo)], dma_engine_mask=bits(engines(on & ~up)[:NX_ENG]), remote_sem=T.sem["hn"], srcs=[n], dsts=[n]),
        RemoteDMATransfer(dst_ids=[dst_id(mate, core, topo)], dma_engine_mask=bits(engines(up)[:NX_ENG]), remote_sem=T.sem["nxp"], srcs=[n], dsts=[n]),
    ], local_sem=T.sem["ls"])
    tr = []
    for k in range(4):
        need("g", "x%d" % k, 16)
        q = T.XALL[:, 1024 * r + 256 * k:1024 * r + 256 * k + 256]
        tr.append(RemoteDMATransfer(dst_ids=[dst_id(hs[k], core, topo)], dma_engine_mask=bits(engines(on)[4 * k:4 * k + 4]),
                                    remote_sem=T.sem["hx"], srcs=[q], dsts=[q]))
    g.remote_dma_fused(tr, local_sem=T.sem["ls"])
    q = T.XALL[:, 1024 * r:1024 * r + 512]
    g.remote_dma_fused([RemoteDMATransfer(dst_ids=[dst_id(mate, core, topo)], dma_engine_mask=up, remote_sem=T.sem["xr"], srcs=[q], dsts=[q])],
                       local_sem=T.sem["ls"])
    loc = 2 * NX_ENG + 16 + 8
    op("g", lambda: g.iota(at("IL", 0, 512), [[1, 512]], 0, 0), [], [("IL", 0, 512)])

    ashr, band = Op.arith_shift_right, Op.bitwise_and
    ms(("LQ", 0, 512), 0.0)
    ms(("LP", 0, 512), 0.0)
    ms(("ONE", 0, 128), 1.0)
    ts(("IP", 2, 3), ("IP", 0, 1), 4, None, ashr)
    ts(("IP", 3, 4), ("IP", 0, 1), 15, None, band)
    ts(("IP", 4, 5), ("IP", 0, 1), 7, None, band)
    ts(("IP", 5, 6), ("IP", 0, 1), 3, 1, ashr, band)
    ts(("IP", 6, 7), ("IP", 0, 1), 2, 3, ashr, band)
    for t in range(7):
        ts(("IP", 8 + t, 9 + t), ("IP", 0, 1), t, 1, ashr, band)
    tc(("PF", 0, 5), ("IP", 2, 7))
    tc(("EXP", 0, 32), ("IA", 0, 32))
    ts(("PF", 5, 6), ("PF", 3, 4), -1.0, 1.0, Op.mult, Op.add)
    ts(("PF", 17, 18), ("PF", 4, 5), -512.0, 1536.0, Op.mult, Op.add)
    ts(("DM", 0, 512), ("IQ", 0, 512), ("PF", 1), None, Op.is_equal)
    ts(("PF", 15, 16), ("PF", 2, 3), -1.0, 0.5, Op.mult, Op.add)
    ts(("PF", 7, 8), ("PF", 0, 1), 512.0, ("PF", 1), Op.mult, Op.add)
    ts(("PF", 8, 15), ("IP", 8, 15), -512.0, 512.0, Op.mult, Op.add)
    ts(("PF", 26, 27), ("PF", 2, 3), 0.0, 6.0, Op.is_equal, Op.mult)
    ts(("PF", 25, 26), ("PF", 17, 18), 512.0, None, Op.add)
    ts(("PF", 18, 25), ("PF", 8, 15), ("PF", 17), None, Op.add)
    ts(("PF", 28, 29), ("PF", 26, 27), 1.0, ("PF", 3), Op.add, Op.mult)
    ts(("PF", 27, 28), ("PF", 26, 27), 1.0 / 3.0, ("PF", 5), Op.mult, Op.mult)
    ts(("PF", 29, 30), ("PF", 3, 4), 255.5, 0.5, Op.mult, Op.add)
    ts(("MG", 0, 128), ("IA", 0, 128), 4, None, ashr)
    ts(("M8", 0, 128), ("IA", 0, 128), 7, None, band)
    ts(("IM", 0, 128), ("IA", 0, 128), 7.0, None, Op.add)
    ts(("MT", 0, 128), ("IA", 0, 128), 3, 1, ashr, band)
    ts(("K3", 0, 128), ("IA", 0, 128), 3, None, band)
    ts(("BD", 0, 128), ("MG", 0, 128), ("PF", 0), None, Op.is_equal)
    ts(("IM", 0, 128), ("IM", 0, 128), 7, None, band)
    ts(("SN", 0, 128), ("M8", 0, 128), 0.0, 2.0, Op.is_equal, Op.mult)
    ac(("BL", 0, 128), ("BD", 0, 128), scale=("PF", 5))
    ts(("T1", 0, 128), ("M8", 0, 128), ("PF", 0), None, Op.is_equal)
    ts(("SN", 0, 128), ("SN", 0, 128), -1.0, None, Op.add)
    ts(("T2", 0, 128), ("IM", 0, 128), ("PF", 0), None, Op.is_equal)
    ts(("T3", 0, 128), ("MT", 0, 128), ("PF", 3), None, Op.is_equal)
    tt(("T2", 0, 128), ("T2", 0, 128), ("SN", 0, 128), Op.mult)
    ac(("LG", 0, 128), ("BD", 0, 128), scale=("PF", 3))
    tt(("T1", 0, 128), ("T1", 0, 128), ("T2", 0, 128), Op.add)
    tt(("LWH", 0, 128), ("T1", 0, 128), ("MT", 0, 128), Op.mult)
    tt(("LW", 0, 128), ("T1", 0, 128), ("T3", 0, 128), Op.mult)
    tt(("LWL", 0, 128), ("T1", 0, 128), ("LWH", 0, 128), Op.subtract)
    ac(("LV", 0, 128), ("LW", 0, 128), scale=0.5)
    ac(("LH", 0, 128), ("LG", 0, 128), scale=0.5)
    ts(("D0", 0, 128), ("K3", 0, 128), ("PF", 4), 16896.0, Op.is_equal, Op.mult)
    ts(("JI", 0, 32), ("IA", 0, 32), 16.0, ("PF", 7), Op.mult, Op.add)
    ts(("EG", 0, 8), ("IA", 0, 8), ("PF", 0), None, Op.is_equal)
    ts(("D0", 0, 128), ("D0", 0, 128), -512.0, None, Op.add)
    ts(("SS", 0, 128), ("IQ", 0, 128), ("PF", 1), None, Op.is_equal)
    ts(("P8X", 0, 16), ("IA", 0, 16), 0.0, ("PF", 2), Op.mult, Op.add)
    ts(("R8", 0, 8), ("EG", 0, 8), ("PF", 29), None, Op.mult)
    ts(("WINA", 512, 1024), ("IL", 0, 512), ("PF", 27), ("PF", 28), Op.mult, Op.add)
    for b, f in (("LQ", 1.0), ("LP", 0.5)):
        for k in range(4):
            op("a", lambda: g.scalar.activation(T[b][:, 128 * k + k:128 * k + 128:4], T.BL[:, k:128:4], Act.Copy, scale=f),
               [("BL", 0, 128)], [(b, 128 * k, 128 * k + 128)])
    for k in range(8):
        ac(("SG", 128 * k, 128 * k + 128), ("SS", 0, 128), scale=("EG", k))
    ac(("WINB", 512, 1024), ("WINA", 512, 1024))

    def gat(out, win, off, m):
        op("v", lambda: g.vector.tensor_tensor(at(*out), T[win[0]][:, win[1]:win[2]].indirect(at(*off)), at(*m), Op.mult),
           [win, off, m], [out])

    def mask0(out, i0):
        ts(out, i0, ("PF", 2), 0.5, Op.is_ge, Op.subtract)

    def mask1(out, i0):
        op("a", lambda: g.scalar.activation(at(*out), at(*i0), Act.Sign, bias=T.PF[:, 15:16]), [i0, ("PF", 15, 16)], [out])

    def blk(s):
        return ("NXT", 32 * s, 32 * s + 32)
    tt(("VA", 0, 32), blk(r), blk(rm), Op.add, ext=(("nl", 32), ("nxp", NX_ENG), ("cv", nz)))
    tt(("VB", 0, 32), blk(ro[0]), blk(ro[1]), Op.add, ext=(("nxo", 16),))
    tt(("VV", 0, 32), ("VA", 0, 32), ("VB", 0, 32), Op.add)
    ts(("VH", 0, 32), ("VV", 0, 32), 9, None, ashr)
    ts(("VL", 0, 32), ("VV", 0, 32), 511, None, band)
    tt(("EQ", 0, 32), ("VV", 0, 32), ("JI", 0, 32), Op.is_equal)
    gat(("X", 0, 512), ("VH", 0, 32), ("EXP", 0, 32), ("DM", 0, 512))
    tt(("ET", 0, 32), ("EQ", 0, 32), ("JI", 0, 32), Op.mult)
    tc(("OFF", 0, 32), ("VL", 0, 32))
    gat(("XE", 0, 256), ("VL", 0, 32), ("EXP", 0, 16), ("DM", 0, 256))
    tt(("ED", 0, 32), ("VV", 0, 32), ("ET", 0, 32), Op.subtract)
    gat(("XE", 256, 512), ("VL", 0, 32), ("EXP", 16, 32), ("DM", 256, 512))
    op("v", lambda: g.vector.tensor_reduce(at("HS", 0, 1), at("ED", 0, 32), AxisListType.X, Op.add), [("ED", 0, 32)], [("HS", 0, 1)])
    for c in (1, 0):
        mm(("G%d" % c, 0, 256), ("BD", 0, 128), ("X", 256 * c, 256 * c + 256), True, True)
    for c in range(2):
        mm(("W%d" % c, 0, 256), ("LWH", 0, 128), ("X", 256 * c, 256 * c + 256), True, False)
    for c in range(2):
        mm(("W%d" % c, 0, 256), ("LWL", 0, 128), ("XE", 256 * c, 256 * c + 256), False, True)
    mm(("HD", 0, 1), ("ONE", 0, 128), ("HS", 0, 1), True, True)
    mask1(("M", 256, 512), ("G1", 0, 256))
    for c in range(2):
        ac(("WINA", 256 * c, 256 * c + 256), ("W%d" % c, 0, 256))
    mask0(("M", 0, 256), ("G0", 0, 256))
    ts(("HI", 0, 1), ("HD", 0, 1), -1.0, float(4096 * 4095 // 2), Op.mult, Op.add)
    ts(("HI", 1, 2), ("HI", 0, 1), 9, None, ashr)
    ts(("HI", 2, 3), ("HI", 0, 1), 511, None, band)
    ts(("HS", 1, 2), ("HI", 1, 2), 0.5, None, Op.add)
    ts(("OFF", 32, 33), ("HI", 2, 3), ("PF", 8), None, Op.add)
    op("a", lambda: g.scalar.activation(T.M[:, 512:528], T.P8X[:, 0:16], Act.Sign, bias=T.HS[:, 1:2], scale=-1.0),
       [("P8X", 0, 16), ("HS", 1, 2)], [("M", 512, 528)])

    def sums(i, a, b, lq):
        for k in range(4):
            mm(("OF%d" % i, 0, (b - a) // 4), (lq, 128 * k, 128 * k + 128), ("X", a + k, b), k == 0, k == 3, sr=4)

    def scan(i, n):
        op("v", lambda: g.vector.tensor_tensor_scan(at("S%d" % i, 0, n), at("D0", 0, n), at("OF%d" % i, 0, n), 0.0, Op.add, Op.min),
           [("D0", 0, n), ("OF%d" % i, 0, n)], [("S%d" % i, 0, n)])

    def pick(i, c0, c1, o0, col):
        op("v", lambda: g.vector.tensor_scalar(at("OFF", o0, o0 + c1 - c0), at("S%d" % i, 4 * c0 + 3, 4 * c1, 4), at("PF", col, col + 1), None, Op.add),
           [("S%d" % i, 4 * c0, 4 * c1), ("PF", col, col + 1)], [("OFF", o0, o0 + c1 - c0)])

    cw = 1
    for t in range(12):
        win, nxt = (("WINA", "WINB") if t % 2 == 0 else ("WINB", "WINA"))
        wb = 512 + 16 * cw
        app = t in (7, 8, 9)
        o = 32 + cw if app else 32
        mo = 512 + 16 * (o - 32)
        u = t + 1
        hold = u >= 10 and not (r >> (u - 10) & 1)
        wcol = 18 + u if u <= 6 else 25 if hold else 17
        if t == 11:
            gat(("X", 512, wb), (win, 0, 1024), ("OFF", 32, 32 + cw), ("M", 512, wb))
            break
        gat(("X", 0, 256), (win, 0, 512), ("OFF", 0, 16), ("M", 0, 256))
        if t == 10:
            gat(("X", 256, 512), (win, 0, 512), ("OFF", 16, 32), ("M", 256, 512))
            gat(("X", 512, wb), (win, 0, 1024), ("OFF", 32, 32 + cw), ("M", 512, wb))
            mm(("W0", 0, 256), ("LW", 0, 128), ("X", 0, 256), True, True)
            ac((nxt, 0, 256), ("W0", 0, 256))
            mm(("W1", 0, 256), ("LV", 0, 128), ("X", 256, 512), True, True)
            ac((nxt, 256, 512), ("W1", 0, 256))
            sums(1, 512, wb, "LP")
            mm(("G1", 0, wb - 512), ("LH", 0, 128), ("X", 512, wb), True, True)
            scan(1, 4 * cw)
            mask1(("M", 512, wb), ("G1", 0, wb - 512))
            pick(1, 0, cw, 32, wcol)
            continue
        gat(("X", 256, wb), (win, 0, 1024), ("OFF", 16, 32 + cw), ("M", 256, wb))
        mm(("W0", 0, 256), ("LW", 0, 128), ("X", 0, 256), True, True)
        sums(0, 0, 256, "LQ")
        mm(("G0", 0, 256), ("LG", 0, 128), ("X", 0, 256), True, True)
        mm(("W1", 0, 256), ("LV", 0, 128), ("X", 256, 512), True, True)
        sums(1, 256, wb, "LP")
        mm(("G1", 0, wb - 256), ("LH", 0, 128), ("X", 256, wb), True, True)
        ac((nxt, 0, 256), ("W0", 0, 256))
        ac((nxt, 256, 512), ("W1", 0, 256))
        scan(0, 64)
        mask0(("M", 0, 256), ("G0", 0, 256))
        scan(1, (wb - 256) // 4)
        pick(0, 0, 16, 0, 17)
        if wcol == 17 and o == 32:
            pick(1, 0, 16 + cw, 16, 17)
        else:
            pick(1, 0, 16, 16, 17)
            pick(1, 16, 16 + cw, o, wcol)
        if app and hold:
            ts(("OFF", 32, 32 + cw), ("OFF", 32, 32 + cw), 512.0, None, Op.add)
        if app:
            mask1(("M", 256, 512), ("G1", 0, 256))
            mask1(("M", mo, mo + 16 * cw), ("G1", 256, 256 + 16 * cw))
            cw *= 2
        else:
            mask1(("M", 256, wb), ("G1", 0, wb - 256))
    mm(("HD", 0, 8), ("X", 512, 640), ("R8", 0, 8), True, True)
    ts(("VF", 0, 8), ("HD", 0, 8), -2048.0, None, Op.add)
    for k in range(8):
        mm(("G0", 8 * k, 8 * k + 8), ("SG", 128 * k, 128 * k + 128), ("VF", 0, 8), True, True)
    ts(("OFY", 0, 64), ("G0", 0, 64), 2048.0, None, Op.add)
    xs = (("x0", 16), ("x1", 16), ("x2", 16), ("x3", 16), ("xr", 8 * 3 + 8 * 4 * 2))
    for c, q in ((0, "v"), (2, "a"), (1, "v"), (3, "a")):
        a, b = 256 * c, 256 * c + 256
        if q == "v":
            op("v", lambda: g.vector.tensor_copy(T.YB[:, a:b], T.XALL[:, 0:4096].indirect(T.OFY[:, 16 * c:16 * c + 16])),
               [("OFY", 0, 64)], [("YB", a, b)], xs)
        else:
            op("a", lambda: g.scalar.activation(T.YB[:, a:b], T.XALL[:, 0:4096].indirect(T.OFY[:, 16 * c:16 * c + 16]), Act.Copy),
               [("OFY", 0, 64)], [("YB", a, b)], xs)
        if c == 3:
            need("a", "c" + q, cnt[q])
            g.scalar.dma_start(T.y[:, a:b], T.YB[:, a:b]).then_inc(T.sem["ys"], 16)
        else:
            need("s", "c" + q, cnt[q])
            g.sync.dma_start(T.y[:, a:b], T.YB[:, a:b]).then_inc(T.sem["ys"], 16)
    g.wait_ge(T.sem["ls"], loc)
    for e in "vpa":
        need("g", "c" + e, cnt[e])
    g.wait_ge(T.sem["cg"], cnt["g"])
    g.wait_ge(T.sem["ys"], 64)
